import numpy as np
import ml_dtypes

BF16 = ml_dtypes.bfloat16


def bf(x):
    return np.asarray(x, np.float32).astype(BF16)


def f32(x):
    return np.asarray(x, np.float32)


def f64(x):
    return np.asarray(x).astype(np.float64)


def striped(idx):
    return np.tile(idx.reshape(-1, 16).T, (8, 1))


S, K, N, V, D, H, O = 2048, 128, 768, 384, 2, 256, 128


def setup_inputs():
    return {"table": bf(np.random.standard_normal((K, S))), "w": bf(np.random.standard_normal((D, K, H)) / np.sqrt(D * K)), "b": f32(0.5 * np.random.standard_normal((H, 1))), "w2": bf(np.random.standard_normal((H, O)) / np.sqrt(H)), "offs": striped(np.random.permutation(S)[:N])}


def reference(table, w, b, w2, offs):
    idx = offs[:16].T.reshape(-1)
    x = f64(table)[:, idx]
    t = sum(f64(w)[d].T @ x[:, d * V : (d + 1) * V] for d in range(D)) + f64(b)
    t = np.maximum(t, 0.0)
    return f64(w2).T @ t

@@ -1,0 +1,49 @@
+import concourse.mybir as mybir
+
+P = 128
+S, V, D, H, O = 2048, 384, 2, 256, 128
+BLOCKS = H // P
+COLS = V // 16
+
+FLOPS = 2 * V * (D * P * H + H * O)
+
+BF16, F32, U16 = mybir.dt.bfloat16, mybir.dt.float32, mybir.dt.uint16
+ALU = mybir.AluOpType
+
+
+def tile_rows_edge2_relu_sub_kernel(tc, table, w, b, w2, offs, out):
+    nc = tc.nc
+    with (
+        tc.tile_pool(name="held", bufs=1) as held,
+        tc.psum_pool(name="psum", bufs=1) as psum,
+    ):
+        offsets = held.tile([P, D * COLS], U16, name="offsets")
+        nodes = held.tile([P, S], BF16, name="nodes")
+        w1_sb = held.tile([P, D, H], BF16, name="w1_sb")
+        w2_sb = held.tile([P, BLOCKS, O], BF16, name="w2_sb")
+        bias = held.tile([P, BLOCKS], F32, name="bias")
+
+        nc.sync.dma_start(offsets[:], offs)
+        nc.sync.dma_start(nodes[:], table)
+        nc.scalar.dma_start(w1_sb[:], w.rearrange("d k h -> k d h"))
+        nc.scalar.dma_start(bias[:], b.rearrange("(a p) o -> p (a o)", p=P))
+        nc.scalar.dma_start(w2_sb[:], w2.rearrange("(a p) o -> p a o", p=P))
+
+        hidden = []
+        for a in range(BLOCKS):
+            pre = psum.tile([P, V], F32, name=f"pre{a}")
+            for d in range(D):
+                picked = nodes[:].indirect(offsets[:, d * COLS:(d + 1) * COLS])
+                nc.tensor.matmul(pre[:], w1_sb[:, d, a * P:(a + 1) * P], picked,
+                                 start=(d == 0), stop=(d == D - 1))
+            h = held.tile([P, V], BF16, name=f"h{a}")
+            nc.vector.tensor_scalar(h[:], pre[:], bias[:, a:a + 1], 0.0, ALU.add, ALU.max)
+            hidden.append(h)
+
+        res = psum.tile([P, V], F32, name="res")
+        for a in range(BLOCKS):
+            nc.tensor.matmul(res[:], w2_sb[:, a, :], hidden[a][:],
+                             start=(a == 0), stop=(a == BLOCKS - 1))
+        staged = held.tile([P, V], F32, name="staged")
+        nc.vector.tensor_copy(staged[:], res[:])
+        nc.sync.dma_start(out, staged[:])

@@ -4,6 +4,7 @@ P = 128
 S, V, D, H, O = 2048, 384, 2, 256, 128
 BLOCKS = H // P
 COLS = V // 16
+HALF = V // 2
 
 FLOPS = 2 * V * (D * P * H + H * O)
 
@@ -23,11 +24,18 @@ def tile_rows_edge2_relu_sub_kernel(tc, table, w, b, w2, offs, out):
         w2_sb = held.tile([P, BLOCKS, O], BF16, name="w2_sb")
         bias = held.tile([P, BLOCKS], F32, name="bias")
 
-        nc.sync.dma_start(offsets[:], offs)
         nc.sync.dma_start(nodes[:], table)
         nc.scalar.dma_start(w1_sb[:], w.rearrange("d k h -> k d h"))
-        nc.scalar.dma_start(bias[:], b.rearrange("(a p) o -> p (a o)", p=P))
-        nc.scalar.dma_start(w2_sb[:], w2.rearrange("(a p) o -> p a o", p=P))
+        nc.sync.dma_start(offsets[:], offs)
+        nc.sync.dma_start(bias[:], b.rearrange("(a p) o -> p (a o)", p=P))
+        nc.sync.dma_start(w2_sb[:], w2.rearrange("(a p) o -> p a o", p=P))
+
+        warm_in = held.tile([P, 1], F32, name="warm_in")
+        warm_out = held.tile([P, 1], F32, name="warm_out")
+        nc.vector.memset(warm_in[:], 0.0)
+        nc.scalar.copy(warm_out[:], warm_in[:])
+
+        halves = [slice(0, HALF), slice(HALF, V)]
 
         hidden = []
         for a in range(BLOCKS):
@@ -36,14 +44,19 @@ def tile_rows_edge2_relu_sub_kernel(tc, table, w, b, w2, offs, out):
                 picked = nodes[:].indirect(offsets[:, d * COLS:(d + 1) * COLS])
                 nc.tensor.matmul(pre[:], w1_sb[:, d, a * P:(a + 1) * P], picked,
                                  start=(d == 0), stop=(d == D - 1))
-            h = held.tile([P, V], BF16, name=f"h{a}")
-            nc.vector.tensor_scalar(h[:], pre[:], bias[:, a:a + 1], 0.0, ALU.add, ALU.max)
+            h = [held.tile([P, HALF], BF16, name=f"h{a}_{c}") for c in range(2)]
+            for c, cols in enumerate(halves):
+                nc.vector.tensor_scalar(h[c][:], pre[:, cols], bias[:, a:a + 1], 0.0,
+                                        ALU.add, ALU.max)
             hidden.append(h)
 
-        res = psum.tile([P, V], F32, name="res")
+        res = [psum.tile([P, HALF], F32, name=f"res{c}") for c in range(2)]
         for a in range(BLOCKS):
-            nc.tensor.matmul(res[:], w2_sb[:, a, :], hidden[a][:],
-                             start=(a == 0), stop=(a == BLOCKS - 1))
-        staged = held.tile([P, V], F32, name="staged")
-        nc.vector.tensor_copy(staged[:], res[:])
-        nc.sync.dma_start(out, staged[:])
+            for c in range(2):
+                nc.tensor.matmul(res[c][:], w2_sb[:, a, :], hidden[a][c][:],
+                                 start=(a == 0), stop=(a == BLOCKS - 1))
+        staged = [held.tile([P, HALF], F32, name=f"staged{c}") for c in range(2)]
+        nc.scalar.copy(staged[0][:], res[0][:])
+        nc.sync.dma_start(out[:, halves[0]], staged[0][:])
+        nc.vector.tensor_copy(staged[1][:], res[1][:])
+        nc.sync.dma_start(out[:, halves[1]], staged[1][:])

@@ -20,15 +20,15 @@ def tile_rows_edge2_relu_sub_kernel(tc, table, w, b, w2, offs, out):
     ):
         offsets = held.tile([P, D * COLS], U16, name="offsets")
         nodes = held.tile([P, S], BF16, name="nodes")
-        w1_sb = held.tile([P, D, H], BF16, name="w1_sb")
+        w1_sb = held.tile([P, D, P, BLOCKS], BF16, name="w1_sb")
         w2_sb = held.tile([P, BLOCKS, O], BF16, name="w2_sb")
         bias = held.tile([P, BLOCKS], F32, name="bias")
 
         nc.sync.dma_start(nodes[:], table)
-        nc.scalar.dma_start(w1_sb[:], w.rearrange("d k h -> k d h"))
+        nc.scalar.dma_start(w1_sb[:], w.rearrange("d k (p a) -> k d p a", a=BLOCKS))
         nc.sync.dma_start(offsets[:], offs)
-        nc.sync.dma_start(bias[:], b.rearrange("(a p) o -> p (a o)", p=P))
-        nc.sync.dma_start(w2_sb[:], w2.rearrange("(a p) o -> p a o", p=P))
+        nc.sync.dma_start(bias[:], b.rearrange("(p a) o -> p (a o)", a=BLOCKS))
+        nc.sync.dma_start(w2_sb[:], w2.rearrange("(p a) o -> p a o", a=BLOCKS))
 
         warm_in = held.tile([P, 1], F32, name="warm_in")
         warm_out = held.tile([P, 1], F32, name="warm_out")
@@ -42,7 +42,7 @@ def tile_rows_edge2_relu_sub_kernel(tc, table, w, b, w2, offs, out):
             pre = psum.tile([P, V], F32, name=f"pre{a}")
             for d in range(D):
                 picked = nodes[:].indirect(offsets[:, d * COLS:(d + 1) * COLS])
-                nc.tensor.matmul(pre[:], w1_sb[:, d, a * P:(a + 1) * P], picked,
+                nc.tensor.matmul(pre[:], w1_sb[:, d, :, a], picked,
                                  start=(d == 0), stop=(d == D - 1))
             h = [held.tile([P, HALF], BF16, name=f"h{a}_{c}") for c in range(2)]
             for c, cols in enumerate(halves):

import concourse.mybir as mybir

P = 128
S, V, D, H, O = 2048, 384, 2, 256, 128
BLOCKS = H // P
COLS = V // 16
HALF = V // 2

FLOPS = 2 * V * (D * P * H + H * O)

BF16, F32, U16 = mybir.dt.bfloat16, mybir.dt.float32, mybir.dt.uint16
ALU = mybir.AluOpType


def tile_rows_edge2_relu_sub_kernel(tc, table, w, b, w2, offs, out):
    nc = tc.nc
    with (
        tc.tile_pool(name="held", bufs=1) as held,
        tc.psum_pool(name="psum", bufs=1) as psum,
    ):
        offsets = held.tile([P, D * COLS], U16, name="offsets")
        nodes = held.tile([P, S], BF16, name="nodes")
        w1_sb = held.tile([P, D, P, BLOCKS], BF16, name="w1_sb")
        w2_sb = held.tile([P, BLOCKS, O], BF16, name="w2_sb")
        bias = held.tile([P, BLOCKS], F32, name="bias")

        nc.sync.dma_start(nodes[:], table)
        nc.scalar.dma_start(w1_sb[:], w.rearrange("d k (p a) -> k d p a", a=BLOCKS))
        nc.sync.dma_start(offsets[:], offs)
        nc.sync.dma_start(bias[:], b.rearrange("(p a) o -> p (a o)", a=BLOCKS))
        nc.sync.dma_start(w2_sb[:], w2.rearrange("(p a) o -> p a o", a=BLOCKS))

        warm_in = held.tile([P, 1], F32, name="warm_in")
        warm_out = held.tile([P, 1], F32, name="warm_out")
        nc.vector.memset(warm_in[:], 0.0)
        nc.scalar.copy(warm_out[:], warm_in[:])

        halves = [slice(0, HALF), slice(HALF, V)]

        hidden = []
        for a in range(BLOCKS):
            pre = psum.tile([P, V], F32, name=f"pre{a}")
            for d in range(D):
                picked = nodes[:].indirect(offsets[:, d * COLS:(d + 1) * COLS])
                nc.tensor.matmul(pre[:], w1_sb[:, d, :, a], picked,
                                 start=(d == 0), stop=(d == D - 1))
            h = [held.tile([P, HALF], BF16, name=f"h{a}_{c}") for c in range(2)]
            for c, cols in enumerate(halves):
                nc.vector.tensor_scalar(h[c][:], pre[:, cols], bias[:, a:a + 1], 0.0,
                                        ALU.add, ALU.max)
            hidden.append(h)

        res = [psum.tile([P, HALF], F32, name=f"res{c}") for c in range(2)]
        for a in range(BLOCKS):
            for c in range(2):
                nc.tensor.matmul(res[c][:], w2_sb[:, a, :], hidden[a][c][:],
                                 start=(a == 0), stop=(a == BLOCKS - 1))
        staged = [held.tile([P, HALF], F32, name=f"staged{c}") for c in range(2)]
        nc.scalar.copy(staged[0][:], res[0][:])
        nc.sync.dma_start(out[:, halves[0]], staged[0][:])
        nc.vector.tensor_copy(staged[1][:], res[1][:])
        nc.sync.dma_start(out[:, halves[1]], staged[1][:])
